import numpy as np
import ml_dtypes


def mxq(x, axis, fmt="e4m3"):
    dtype, down = {"e4m3": (ml_dtypes.float8_e4m3fn, 7), "e5m2": (ml_dtypes.float8_e5m2, 14)}[fmt]
    v = np.moveaxis(np.asarray(x, np.float32).astype(ml_dtypes.bfloat16).astype(np.float64), axis, -1)
    blocks = v.reshape(v.shape[:-1] + (-1, 32))
    amax = np.abs(blocks).max(-1, keepdims=True)
    byte = np.maximum(np.where(amax > 0, np.frexp(amax)[1] - 1 + 127, 0) - down, 1)
    scale = np.exp2(byte - 127.0)
    codes = (blocks / scale).astype(np.float32).astype(dtype).astype(np.float64)
    return np.moveaxis((codes * scale).reshape(v.shape), -1, axis)


WIDE = False


def mx_kscale(k):
    if not WIDE:
        return np.ones(k)
    levels = np.array([30, -30])
    if k % 512:
        return np.exp2(np.random.permutation(np.resize(levels, k // 32))).repeat(32)
    a = np.empty((k // 512, 16))
    for p in range(k // 512):
        a[p, :8] = np.random.permutation(np.resize(levels, 8))
        for g in range(8):
            far = levels[np.abs(levels - a[p, g]) >= 10]
            a[p, g + 8] = far[np.random.randint(len(far))]
    return np.exp2(a.ravel()).repeat(32)


def f64(x):
    return np.asarray(x).astype(np.float64)


def striped(idx):
    return np.tile(np.asarray(idx).reshape(-1, 16).T, (8, 1)).astype(np.uint16)


def unstriped(offs):
    return offs[:16].T.reshape(-1).astype(np.int64)


K, J, N, T, B, V, Q = 256, 1024, 256, 2048, 128, 2048, 1024


def setup_inputs():
    n = np.random.standard_normal
    idx = np.random.permutation(T)[:J]
    idx2 = np.random.permutation(V)[:J]
    idx3 = np.random.permutation(Q)[:N]
    fj = mx_kscale(J)
    return {
        "xf": (n((K, T))).astype(np.float32),
        "ra": (np.random.uniform(0.5, 1.5, (1, J)) * fj).astype(np.float32),
        "gt": (n((N, V)) * np.exp(0.5 * n((1, V)))).astype(np.float32),
        "rb": (np.random.uniform(0.5, 1.5, (1, J)) / fj).astype(np.float32),
        "sv": (n((N, V))).astype(np.float32),
        "old": (0.5 * n((K, Q))).astype(np.float32),
        "offs": striped(idx),
        "offs2": striped(idx2),
        "offs3": striped(idx3),
    }


def reference(xf, ra, gt, rb, sv, old, offs, offs2, offs3):
    idx = unstriped(offs)
    idx2 = unstriped(offs2)
    idx3 = unstriped(offs3)
    xg = f64(xf)[:, idx]
    g1 = xg.reshape(K, B, J // B).mean(axis=2)
    g2 = np.repeat(g1, J // B, axis=1)
    us = (xg - g2) * f64(ra)
    uj = us.T
    gs = f64(gt)[:, idx2] * np.maximum(f64(sv)[:, idx2], 0.0) * f64(rb)
    gj = gs.T
    ujq = mxq(uj, 0, "e5m2")
    gjq = mxq(gj, 0, "e5m2")
    w = ujq.T @ gjq
    wp = np.zeros((K, Q))
    wp[:, idx3] = w
    y = 0.04 * wp + f64(old)
    return y

@@ -1,0 +1,189 @@
+from contextlib import ExitStack
+
+import concourse.mybir as mybir
+from concourse.masks import make_identity
+
+K, J, N, T, V, Q = 256, 1024, 256, 2048, 2048, 1024
+FLOPS = 2 * K * J * N
+
+F32 = mybir.dt.float32
+BF16 = mybir.dt.bfloat16
+U32 = mybir.dt.uint32
+U16 = mybir.dt.uint16
+U8 = mybir.dt.uint8
+E5M2X4 = mybir.dt.float8_e5m2_x4
+ALU = mybir.AluOpType
+COPY = mybir.ActivationFunctionType.Copy
+AXIS_X = mybir.AxisListType.X
+
+P = 128
+PACK = 4
+PASS = P * PACK
+PASSES = J // PASS
+GROUP = 8
+LANES = 16
+STEP = 0.04
+HALF = Q // 2
+
+
+def tile_list_moment_centred_saved_placed_kernel(tc, xf, ra, gt, rb, sv, old, offs, offs2, offs3, out):
+    nc = tc.nc
+    with ExitStack() as ctx:
+        held = ctx.enter_context(tc.tile_pool(name="held", bufs=1))
+        turn = ctx.enter_context(tc.psum_pool(name="turn", bufs=5))
+        sums_psum = ctx.enter_context(tc.psum_pool(name="sums_psum", bufs=1))
+
+        def rows(i):
+            return slice(i * P, (i + 1) * P)
+
+        def entries(lst, start, count):
+            return lst[:, start // LANES:(start + count) // LANES]
+
+        x_list = held.tile([P, J // LANES], U16, name="x_list")
+        g_list = held.tile([P, J // LANES], U16, name="g_list")
+        place_list = held.tile([P, N // LANES], U16, name="place_list")
+        x_win = [held.tile([P, T], F32, name="x_win%d" % i) for i in range(2)]
+        g_win = [held.tile([P, V], F32, name="g_win%d" % i) for i in range(2)]
+        s_win = [held.tile([P, V], F32, name="s_win%d" % i) for i in range(2)]
+        store = [held.tile([P, Q], F32, name="store%d" % i) for i in range(2)]
+        placed = [held.tile([P, Q], F32, name="placed%d" % i) for i in range(2)]
+        ra_slot = held.tile([P, PASSES, PACK], F32, name="ra_slot")
+        rb_slot = held.tile([P, PASSES, PACK], F32, name="rb_slot", tag="gg0")
+        ident = held.tile([P, P], F32, name="ident")
+
+        nc.sync.dma_start(rb_slot[:], rb.rearrange("o (g p t) -> p (o g) t", g=PASSES, t=PACK))
+        nc.sync.dma_start(x_list[:], offs)
+        nc.sync.dma_start(x_win[0][:], xf[rows(0), :])
+        nc.scalar.dma_start(ra_slot[:], ra.rearrange("o (g p t) -> p (o g) t", g=PASSES, t=PACK))
+        nc.sync.dma_start(g_win[0][:], gt[rows(0), :])
+        nc.sync.dma_start(g_list[:], offs2)
+        nc.sync.dma_start(x_win[1][:], xf[rows(1), :])
+        nc.sync.dma_start(s_win[0][:], sv[rows(0), :])
+        nc.sync.dma_start(g_win[1][:], gt[rows(1), :])
+        nc.sync.dma_start(s_win[1][:], sv[rows(1), :])
+        nc.sync.dma_start(place_list[:], offs3)
+        for i in range(2):
+            nc.sync.dma_start(store[i][:], old[rows(i), :])
+
+        make_identity(nc, ident[:])
+        for i in range(2):
+            nc.gpsimd.memset(placed[i][:], 0.0)
+
+        u_codes = [[held.tile([P, P], U32, name="u_codes%d%d" % (i, g), align_bytes=64) for g in range(PASSES)] for i in range(2)]
+        u_scales = [[held.tile([P, P], U8, name="u_scales%d%d" % (i, g), align_bytes=64) for g in range(PASSES)] for i in range(2)]
+        g_codes = [held.tile([P, N], U32, name="g_codes%d" % g, align_bytes=64) for g in range(PASSES)]
+        g_scales = [held.tile([P, N], U8, name="g_scales%d" % g, align_bytes=64) for g in range(PASSES)]
+
+        def work(shape, dtype, tag):
+            return held.tile(shape, dtype, name="work", tag=tag, align_bytes=64)
+
+        def gather(engine, dest, window, lst, g):
+            picked = window[:].indirect(entries(lst, g * PASS, PASS))
+            if engine == "scalar":
+                nc.scalar.activation(dest[:], picked, COPY)
+            else:
+                nc.vector.tensor_copy(dest[:], picked)
+
+        rb_row = []
+        for g in range(PASSES):
+            bank = turn.tile([P, PACK, P], F32, name="bank")
+            for t in range(PACK):
+                nc.tensor.transpose(bank[:, t, :], rb_slot[:, g, t:t + 1].to_broadcast([P, P]), ident[:])
+            row = held.tile([P, PASS], F32, name="rb_row%d" % g)
+            nc.scalar.activation(row[:].rearrange("p (c t) -> p c t", t=PACK), bank[:].rearrange("p t c -> p c t"), COPY)
+            rb_row.append(row)
+
+        def centred_bank(i, g, engine):
+            xg = held.tile([P, PASS], F32, name="xg%d%d" % (i, g))
+            gather(engine, xg, x_win[i], x_list, g)
+            total = held.tile([P, PASS // GROUP, 1], F32, name="total%d%d" % (i, g))
+            nc.vector.tensor_reduce(total[:].rearrange("p b o -> p (b o)"),
+                                    xg[:].rearrange("p (b m) -> p b m", m=GROUP), AXIS_X, ALU.add)
+            minus_mean = held.tile([P, P], F32, name="minus_mean%d%d" % (i, g))
+            nc.vector.tensor_scalar(minus_mean[:].rearrange("p (b u) -> p b u", u=2),
+                                    total[:].to_broadcast([P, PASS // GROUP, 2]), -1.0 / GROUP, None, ALU.mult)
+            bank = turn.tile([P, PACK, P], F32, name="bank")
+            for t in range(PACK):
+                nc.tensor.matmul(bank[:, t, :], xg[:, t:PASS:PACK], ident[:], is_transpose=True,
+                                 start=(t == 0), stop=False)
+            for t in range(PACK):
+                nc.tensor.matmul(bank[:, t, :], minus_mean[:], ident[:], is_transpose=True,
+                                 start=False, stop=(t == PACK - 1))
+            return bank
+
+        def quantise_features(i, g, bank, tag):
+            rounded = work([P, P, PACK], BF16, tag)
+            nc.vector.tensor_tensor(rounded[:], bank[:].rearrange("p t c -> p c t"),
+                                    ra_slot[:, g:g + 1, :].to_broadcast([P, P, PACK]), ALU.mult)
+            nc.vector.quantize_mx(out=u_codes[i][g][:].bitcast(E5M2X4), scales=u_scales[i][g][:],
+                                  in_=rounded[:].rearrange("p c t -> p (c t)"))
+
+        def weighted_gradients(i):
+            fused = work([P, PASS], F32, "gw%d0" % i)
+            nc.vector.tensor_tensor(fused[:], g_win[i][:].indirect(entries(g_list, 0, PASS)), rb_row[0][:], ALU.mult)
+            plain = held.tile([P, PASS], F32, name="gg", tag="gg%d" % i)
+            gather("scalar", plain, g_win[i], g_list, 1)
+            weighted = work([P, PASS], F32, "gw%d1" % i)
+            nc.vector.tensor_tensor(weighted[:], plain[:], rb_row[1][:], ALU.mult)
+            return [fused, weighted]
+
+        def gated_bank(i, g, weighted):
+            sg = work([P, PASS], F32, "sg%d%d" % (i, g))
+            gather("scalar", sg, s_win[i], g_list, g)
+            gated = held.tile([P, PASS], BF16, name="gated%d%d" % (i, g))
+            nc.vector.scalar_tensor_tensor(gated[:], sg[:], 0.0, weighted[:], ALU.max, ALU.mult)
+            pairs = gated[:].bitcast(F32)
+            bank = turn.tile([P, 2, P], F32, name="bank")
+            for u in range(2):
+                nc.tensor.transpose(bank[:, u, :], pairs[:, u:PASS // 2:2], ident[:])
+            return bank
+
+        def quantise_gradients(i, g, bank, tag):
+            rounded = work([P, PASS], BF16, tag)
+            nc.scalar.copy(rounded[:].bitcast(F32).rearrange("p (c u) -> p c u", u=2), bank[:].rearrange("p u c -> p c u"))
+            nc.vector.quantize_mx(out=g_codes[g][:, rows(i)].bitcast(E5M2X4), scales=g_scales[g][:, rows(i)],
+                                  in_=rounded[:])
+
+        def moment(acc, i, n):
+            for g in range(PASSES):
+                nc.tensor.matmul_mx(out=acc, lhsT=u_codes[i][g][:].bitcast(E5M2X4), lhsT_scale=u_scales[i][g][:],
+                                    rhs=g_codes[g][:, rows(n)].bitcast(E5M2X4), rhs_scale=g_scales[g][:, rows(n)],
+                                    start=(g == 0), stop=(g == PASSES - 1))
+
+        x0 = [centred_bank(0, 0, "scalar"), centred_bank(0, 1, "vector")]
+        for g in range(PASSES):
+            quantise_features(0, g, x0[g], "rx0%d" % g)
+        gw0 = weighted_gradients(0)
+        x1 = [centred_bank(1, g, "scalar") for g in range(PASSES)]
+        quantise_features(1, 1, x1[1], "rx11")
+        g0 = [gated_bank(0, g, gw0[g]) for g in range(PASSES)]
+        quantise_gradients(0, 0, g0[0], "sg01")
+        quantise_gradients(0, 1, g0[1], "rg01")
+        gw1 = weighted_gradients(1)
+        g1 = [gated_bank(1, g, gw1[g]) for g in range(PASSES)]
+        quantise_features(1, 0, x1[0], "gw10")
+        for g in range(PASSES):
+            quantise_gradients(1, g, g1[g], "rg1%d" % g)
+
+        early = sums_psum.tile([P, 2, P], F32, name="early")
+        for i in range(2):
+            moment(early[:, i, :], i, 0)
+        w_early = work([P, 2, P], F32, "sg11")
+        nc.scalar.activation(w_early[:], early[:], COPY)
+        for i in range(2):
+            nc.scalar.activation(placed[i][:].indirect(entries(place_list, 0, P)), w_early[:, i, :], COPY)
+        late = [sums_psum.tile([P, P], F32, name="late%d" % i) for i in range(2)]
+        w_late = [held.tile([P, P], F32, name="w_late%d" % i) for i in range(2)]
+        for i in range(2):
+            moment(late[i][:], i, 1)
+        nc.vector.tensor_copy(w_late[0][:], late[0][:])
+        nc.vector.tensor_copy(placed[0][:].indirect(entries(place_list, P, P)), w_late[0][:])
+        nc.scalar.activation(w_late[1][:], late[1][:], COPY)
+        nc.scalar.activation(placed[1][:].indirect(entries(place_list, P, P)), w_late[1][:], COPY)
+
+        for i in range(2):
+            for c in range(0, Q, HALF):
+                cols = slice(c, c + HALF)
+                nc.vector.scalar_tensor_tensor(store[i][:, cols], placed[i][:, cols], STEP, store[i][:, cols],
+                                               ALU.mult, ALU.add)
+                nc.sync.dma_start(out[rows(i), cols], store[i][:, cols])

@@ -24,13 +24,17 @@ GROUP = 8
 LANES = 16
 STEP = 0.04
 HALF = Q // 2
+GROUPS = PASS // GROUP
+WINDOW = 4 * T
+PIECE = 4 * PASS
 
 
 def tile_list_moment_centred_saved_placed_kernel(tc, xf, ra, gt, rb, sv, old, offs, offs2, offs3, out):
     nc = tc.nc
     with ExitStack() as ctx:
         held = ctx.enter_context(tc.tile_pool(name="held", bufs=1))
-        turn = ctx.enter_context(tc.psum_pool(name="turn", bufs=5))
+        reused = ctx.enter_context(tc.tile_pool(name="reused", bufs=1))
+        turn = ctx.enter_context(tc.psum_pool(name="turn", bufs=2))
         sums_psum = ctx.enter_context(tc.psum_pool(name="sums_psum", bufs=1))
 
         def rows(i):
@@ -39,24 +43,28 @@ def tile_list_moment_centred_saved_placed_kernel(tc, xf, ra, gt, rb, sv, old, of
         def entries(lst, start, count):
             return lst[:, start // LANES:(start + count) // LANES]
 
+        def laid(name, shape, dtype, offset):
+            return reused.tile(shape, dtype, name=name, offset=offset, align_bytes=64)
+
         x_list = held.tile([P, J // LANES], U16, name="x_list")
         g_list = held.tile([P, J // LANES], U16, name="g_list")
         place_list = held.tile([P, N // LANES], U16, name="place_list")
-        x_win = [held.tile([P, T], F32, name="x_win%d" % i) for i in range(2)]
-        g_win = [held.tile([P, V], F32, name="g_win%d" % i) for i in range(2)]
-        s_win = [held.tile([P, V], F32, name="s_win%d" % i) for i in range(2)]
+        x_at, g_at, s_at, spare = (0, 2 * WINDOW), (WINDOW, 4 * WINDOW), (3 * WINDOW, 5 * WINDOW), 6 * WINDOW
+        x_win = [laid("x_win%d" % i, [P, T], F32, x_at[i]) for i in range(2)]
+        g_win = [laid("g_win%d" % i, [P, V], F32, g_at[i]) for i in range(2)]
+        s_win = [laid("s_win%d" % i, [P, V], F32, s_at[i]) for i in range(2)]
         store = [held.tile([P, Q], F32, name="store%d" % i) for i in range(2)]
         placed = [held.tile([P, Q], F32, name="placed%d" % i) for i in range(2)]
         ra_slot = held.tile([P, PASSES, PACK], F32, name="ra_slot")
-        rb_slot = held.tile([P, PASSES, PACK], F32, name="rb_slot", tag="gg0")
+        rb_slot = laid("rb_slot", [P, PASSES, PACK], F32, spare)
         ident = held.tile([P, P], F32, name="ident")
 
         nc.sync.dma_start(rb_slot[:], rb.rearrange("o (g p t) -> p (o g) t", g=PASSES, t=PACK))
         nc.sync.dma_start(x_list[:], offs)
         nc.sync.dma_start(x_win[0][:], xf[rows(0), :])
-        nc.scalar.dma_start(ra_slot[:], ra.rearrange("o (g p t) -> p (o g) t", g=PASSES, t=PACK))
         nc.sync.dma_start(g_win[0][:], gt[rows(0), :])
         nc.sync.dma_start(g_list[:], offs2)
+        nc.sync.dma_start(ra_slot[:], ra.rearrange("o (g p t) -> p (o g) t", g=PASSES, t=PACK))
         nc.sync.dma_start(x_win[1][:], xf[rows(1), :])
         nc.sync.dma_start(s_win[0][:], sv[rows(0), :])
         nc.sync.dma_start(g_win[1][:], gt[rows(1), :])
@@ -67,42 +75,34 @@ def tile_list_moment_centred_saved_placed_kernel(tc, xf, ra, gt, rb, sv, old, of
 
         make_identity(nc, ident[:])
         for i in range(2):
-            nc.gpsimd.memset(placed[i][:], 0.0)
+            nc.vector.memset(placed[i][:], 0.0)
 
         u_codes = [[held.tile([P, P], U32, name="u_codes%d%d" % (i, g), align_bytes=64) for g in range(PASSES)] for i in range(2)]
         u_scales = [[held.tile([P, P], U8, name="u_scales%d%d" % (i, g), align_bytes=64) for g in range(PASSES)] for i in range(2)]
-        g_codes = [held.tile([P, N], U32, name="g_codes%d" % g, align_bytes=64) for g in range(PASSES)]
-        g_scales = [held.tile([P, N], U8, name="g_scales%d" % g, align_bytes=64) for g in range(PASSES)]
+        g_codes = [[held.tile([P, P], U32, name="g_codes%d%d" % (i, g), align_bytes=64) for g in range(PASSES)] for i in range(2)]
+        g_scales = [[held.tile([P, P], U8, name="g_scales%d%d" % (i, g), align_bytes=64) for g in range(PASSES)] for i in range(2)]
 
-        def work(shape, dtype, tag):
-            return held.tile(shape, dtype, name="work", tag=tag, align_bytes=64)
-
-        def gather(engine, dest, window, lst, g):
-            picked = window[:].indirect(entries(lst, g * PASS, PASS))
-            if engine == "scalar":
-                nc.scalar.activation(dest[:], picked, COPY)
-            else:
-                nc.vector.tensor_copy(dest[:], picked)
+        def picked(window, lst, g):
+            return window[:].indirect(entries(lst, g * PASS, PASS))
 
         rb_row = []
         for g in range(PASSES):
-            bank = turn.tile([P, PACK, P], F32, name="bank")
+            bank = turn.tile([P, PACK, P], F32, name="wide_bank")
             for t in range(PACK):
                 nc.tensor.transpose(bank[:, t, :], rb_slot[:, g, t:t + 1].to_broadcast([P, P]), ident[:])
             row = held.tile([P, PASS], F32, name="rb_row%d" % g)
             nc.scalar.activation(row[:].rearrange("p (c t) -> p c t", t=PACK), bank[:].rearrange("p t c -> p c t"), COPY)
             rb_row.append(row)
 
-        def centred_bank(i, g, engine):
-            xg = held.tile([P, PASS], F32, name="xg%d%d" % (i, g))
-            gather(engine, xg, x_win[i], x_list, g)
-            total = held.tile([P, PASS // GROUP, 1], F32, name="total%d%d" % (i, g))
+        def group_sums(xg, total):
             nc.vector.tensor_reduce(total[:].rearrange("p b o -> p (b o)"),
                                     xg[:].rearrange("p (b m) -> p b m", m=GROUP), AXIS_X, ALU.add)
-            minus_mean = held.tile([P, P], F32, name="minus_mean%d%d" % (i, g))
+
+        def centred_bank(xg, total, name):
+            minus_mean = held.tile([P, P], F32, name=name)
             nc.vector.tensor_scalar(minus_mean[:].rearrange("p (b u) -> p b u", u=2),
-                                    total[:].to_broadcast([P, PASS // GROUP, 2]), -1.0 / GROUP, None, ALU.mult)
-            bank = turn.tile([P, PACK, P], F32, name="bank")
+                                    total[:].to_broadcast([P, GROUPS, 2]), -1.0 / GROUP, None, ALU.mult)
+            bank = turn.tile([P, PACK, P], F32, name="wide_bank")
             for t in range(PACK):
                 nc.tensor.matmul(bank[:, t, :], xg[:, t:PASS:PACK], ident[:], is_transpose=True,
                                  start=(t == 0), stop=False)
@@ -111,75 +111,103 @@ def tile_list_moment_centred_saved_placed_kernel(tc, xf, ra, gt, rb, sv, old, of
                                  start=False, stop=(t == PACK - 1))
             return bank
 
-        def quantise_features(i, g, bank, tag):
-            rounded = work([P, P, PACK], BF16, tag)
-            nc.vector.tensor_tensor(rounded[:], bank[:].rearrange("p t c -> p c t"),
+        def weigh_features(g, bank, rounded):
+            nc.vector.tensor_tensor(rounded[:].rearrange("p (c t) -> p c t", t=PACK), bank[:].rearrange("p t c -> p c t"),
                                     ra_slot[:, g:g + 1, :].to_broadcast([P, P, PACK]), ALU.mult)
-            nc.vector.quantize_mx(out=u_codes[i][g][:].bitcast(E5M2X4), scales=u_scales[i][g][:],
-                                  in_=rounded[:].rearrange("p c t -> p (c t)"))
 
-        def weighted_gradients(i):
-            fused = work([P, PASS], F32, "gw%d0" % i)
-            nc.vector.tensor_tensor(fused[:], g_win[i][:].indirect(entries(g_list, 0, PASS)), rb_row[0][:], ALU.mult)
-            plain = held.tile([P, PASS], F32, name="gg", tag="gg%d" % i)
-            gather("scalar", plain, g_win[i], g_list, 1)
-            weighted = work([P, PASS], F32, "gw%d1" % i)
-            nc.vector.tensor_tensor(weighted[:], plain[:], rb_row[1][:], ALU.mult)
-            return [fused, weighted]
+        def quantise(codes, scales, rounded):
+            nc.vector.quantize_mx(out=codes[:].bitcast(E5M2X4), scales=scales[:], in_=rounded[:])
 
-        def gated_bank(i, g, weighted):
-            sg = work([P, PASS], F32, "sg%d%d" % (i, g))
-            gather("scalar", sg, s_win[i], g_list, g)
-            gated = held.tile([P, PASS], BF16, name="gated%d%d" % (i, g))
+        def gated_bank(sg, weighted, gated):
             nc.vector.scalar_tensor_tensor(gated[:], sg[:], 0.0, weighted[:], ALU.max, ALU.mult)
             pairs = gated[:].bitcast(F32)
-            bank = turn.tile([P, 2, P], F32, name="bank")
+            bank = turn.tile([P, 2, P], F32, name="pair_bank")
             for u in range(2):
                 nc.tensor.transpose(bank[:, u, :], pairs[:, u:PASS // 2:2], ident[:])
             return bank
 
-        def quantise_gradients(i, g, bank, tag):
-            rounded = work([P, PASS], BF16, tag)
+        def join_pairs(bank, name):
+            rounded = held.tile([P, PASS], BF16, name=name, align_bytes=64)
             nc.scalar.copy(rounded[:].bitcast(F32).rearrange("p (c u) -> p c u", u=2), bank[:].rearrange("p u c -> p c u"))
-            nc.vector.quantize_mx(out=g_codes[g][:, rows(i)].bitcast(E5M2X4), scales=g_scales[g][:, rows(i)],
-                                  in_=rounded[:])
+            return rounded
 
-        def moment(acc, i, n):
+        def moment(i, n):
+            acc = sums_psum.tile([P, P], F32, name="acc%d%d" % (i, n))
             for g in range(PASSES):
-                nc.tensor.matmul_mx(out=acc, lhsT=u_codes[i][g][:].bitcast(E5M2X4), lhsT_scale=u_scales[i][g][:],
-                                    rhs=g_codes[g][:, rows(n)].bitcast(E5M2X4), rhs_scale=g_scales[g][:, rows(n)],
+                nc.tensor.matmul_mx(out=acc[:], lhsT=u_codes[i][g][:].bitcast(E5M2X4), lhsT_scale=u_scales[i][g][:],
+                                    rhs=g_codes[n][g][:].bitcast(E5M2X4), rhs_scale=g_scales[n][g][:],
                                     start=(g == 0), stop=(g == PASSES - 1))
+            return acc
 
-        x0 = [centred_bank(0, 0, "scalar"), centred_bank(0, 1, "vector")]
-        for g in range(PASSES):
-            quantise_features(0, g, x0[g], "rx0%d" % g)
-        gw0 = weighted_gradients(0)
-        x1 = [centred_bank(1, g, "scalar") for g in range(PASSES)]
-        quantise_features(1, 1, x1[1], "rx11")
-        g0 = [gated_bank(0, g, gw0[g]) for g in range(PASSES)]
-        quantise_gradients(0, 0, g0[0], "sg01")
-        quantise_gradients(0, 1, g0[1], "rg01")
-        gw1 = weighted_gradients(1)
-        g1 = [gated_bank(1, g, gw1[g]) for g in range(PASSES)]
-        quantise_features(1, 0, x1[0], "gw10")
-        for g in range(PASSES):
-            quantise_gradients(1, g, g1[g], "rg1%d" % g)
+        def place_on_scalar(i, n):
+            w = held.tile([P, P], F32, name="w%d%d" % (i, n))
+            nc.scalar.activation(w[:], moment(i, n)[:], COPY)
+            nc.scalar.activation(placed[i][:].indirect(entries(place_list, n * P, P)), w[:], COPY)
 
-        early = sums_psum.tile([P, 2, P], F32, name="early")
-        for i in range(2):
-            moment(early[:, i, :], i, 0)
-        w_early = work([P, 2, P], F32, "sg11")
-        nc.scalar.activation(w_early[:], early[:], COPY)
-        for i in range(2):
-            nc.scalar.activation(placed[i][:].indirect(entries(place_list, 0, P)), w_early[:, i, :], COPY)
-        late = [sums_psum.tile([P, P], F32, name="late%d" % i) for i in range(2)]
-        w_late = [held.tile([P, P], F32, name="w_late%d" % i) for i in range(2)]
-        for i in range(2):
-            moment(late[i][:], i, 1)
-        nc.vector.tensor_copy(w_late[0][:], late[0][:])
-        nc.vector.tensor_copy(placed[0][:].indirect(entries(place_list, P, P)), w_late[0][:])
-        nc.scalar.activation(w_late[1][:], late[1][:], COPY)
-        nc.scalar.activation(placed[1][:].indirect(entries(place_list, P, P)), w_late[1][:], COPY)
+        def place_on_vector(i, n):
+            w = held.tile([P, P], F32, name="w%d%d" % (i, n))
+            nc.vector.tensor_copy(w[:], moment(i, n)[:])
+            nc.vector.tensor_copy(placed[i][:].indirect(entries(place_list, n * P, P)), w[:])
+
+        xg0 = [laid("xg00", [P, PASS], F32, spare), held.tile([P, PASS], F32, name="xg01")]
+        total0 = [laid("total00", [P, GROUPS, 1], F32, spare + PIECE), laid("total01", [P, GROUPS, 1], F32, x_at[0] + 3 * PIECE)]
+        nc.scalar.activation(xg0[0][:], picked(x_win[0], x_list, 0), COPY)
+        nc.vector.tensor_copy(xg0[1][:], picked(x_win[0], x_list, 1))
+        for g in (1, 0):
+            group_sums(xg0[g], total0[g])
+        x0 = {g: centred_bank(xg0[g], total0[g], "minus_mean0%d" % g) for g in (1, 0)}
+
+        gw0 = [laid("gw00", [P, PASS], F32, spare + PIECE), laid("gw01", [P, PASS], F32, g_at[0])]
+        gg0 = laid("gg0", [P, PASS], F32, x_at[0])
+        nc.vector.tensor_tensor(gw0[0][:], picked(g_win[0], g_list, 0), rb_row[0][:], ALU.mult)
+        nc.scalar.activation(gg0[:], picked(g_win[0], g_list, 1), COPY)
+        rx0 = [held.tile([P, PASS], BF16, name="rx0%d" % g, align_bytes=64) for g in range(PASSES)]
+        for g in (1, 0):
+            weigh_features(g, x0[g], rx0[g])
+        for g in (1, 0):
+            quantise(u_codes[0][g], u_scales[0][g], rx0[g])
+        nc.vector.tensor_tensor(gw0[1][:], gg0[:], rb_row[1][:], ALU.mult)
+
+        xg1 = [laid("xg1%d" % g, [P, PASS], F32, x_at[0] + (1 + g) * PIECE) for g in range(PASSES)]
+        total1 = [laid("total10", [P, GROUPS, 1], F32, g_at[0] + PIECE), held.tile([P, GROUPS, 1], F32, name="total11")]
+        x1 = []
+        for g in range(PASSES):
+            nc.scalar.activation(xg1[g][:], picked(x_win[1], x_list, g), COPY)
+        for g in range(PASSES):
+            group_sums(xg1[g], total1[g])
+            x1.append(centred_bank(xg1[g], total1[g], "minus_mean1%d" % g))
+
+        sg0 = [laid("sg0%d" % g, [P, PASS], F32, x_at[1] + g * PIECE) for g in range(PASSES)]
+        for g in range(PASSES):
+            nc.scalar.activation(sg0[g][:], picked(s_win[0], g_list, g), COPY)
+        gated0 = [held.tile([P, PASS], BF16, name="gated00"), laid("gated01", [P, PASS], BF16, spare + 3 * PIECE - PIECE // 4)]
+        g0 = [gated_bank(sg0[0], gw0[0], gated0[0])]
+        gw1 = [laid("gw10", [P, PASS], F32, x_at[1]), held.tile([P, PASS], F32, name="gw11")]
+        nc.vector.tensor_tensor(gw1[0][:], picked(g_win[1], g_list, 0), rb_row[0][:], ALU.mult)
+        g0.append(gated_bank(sg0[1], gw0[1], gated0[1]))
+        gg1 = laid("gg1", [P, PASS], F32, x_at[1] + 2 * PIECE)
+        nc.scalar.activation(gg1[:], picked(g_win[1], g_list, 1), COPY)
+        rg0 = [join_pairs(g0[g], "rg0%d" % g) for g in range(PASSES)]
+        rx10 = held.tile([P, PASS], BF16, name="rx10", align_bytes=64)
+        weigh_features(0, x1[0], rx10)
+        nc.vector.tensor_tensor(gw1[1][:], gg1[:], rb_row[1][:], ALU.mult)
+        for g in range(PASSES):
+            quantise(g_codes[0][g], g_scales[0][g], rg0[g])
+        quantise(u_codes[1][0], u_scales[1][0], rx10)
+
+        sg1 = [laid("sg1%d" % g, [P, PASS], F32, spare + (2 + g) * PIECE) for g in range(PASSES)]
+        for g in range(PASSES):
+            nc.scalar.activation(sg1[g][:], picked(s_win[1], g_list, g), COPY)
+        place_on_scalar(0, 0)
+        g1 = [gated_bank(sg1[g], gw1[g], held.tile([P, PASS], BF16, name="gated1%d" % g)) for g in range(PASSES)]
+        for g in range(PASSES):
+            quantise(g_codes[1][g], g_scales[1][g], join_pairs(g1[g], "rg1%d" % g))
+        rx11 = laid("rx11", [P, PASS], BF16, spare + 3 * PIECE)
+        weigh_features(1, x1[1], rx11)
+        quantise(u_codes[1][1], u_scales[1][1], rx11)
+        place_on_vector(0, 1)
+        place_on_scalar(1, 0)
+        place_on_scalar(1, 1)
 
         for i in range(2):
             for c in range(0, Q, HALF):

@@ -77,10 +77,13 @@ def tile_list_moment_centred_saved_placed_kernel(tc, xf, ra, gt, rb, sv, old, of
         for i in range(2):
             nc.vector.memset(placed[i][:], 0.0)
 
-        u_codes = [[held.tile([P, P], U32, name="u_codes%d%d" % (i, g), align_bytes=64) for g in range(PASSES)] for i in range(2)]
-        u_scales = [[held.tile([P, P], U8, name="u_scales%d%d" % (i, g), align_bytes=64) for g in range(PASSES)] for i in range(2)]
-        g_codes = [[held.tile([P, P], U32, name="g_codes%d%d" % (i, g), align_bytes=64) for g in range(PASSES)] for i in range(2)]
-        g_scales = [[held.tile([P, P], U8, name="g_scales%d%d" % (i, g), align_bytes=64) for g in range(PASSES)] for i in range(2)]
+        def operand(name, passes):
+            codes = held.tile([P, passes * P], U32, name=name + "_codes", align_bytes=64)
+            scales = held.tile([P, passes * P], U8, name=name + "_scales", align_bytes=64)
+            return codes, scales
+
+        def pass_of(op, g):
+            return op[0][:, g * P:(g + 1) * P], op[1][:, g * P:(g + 1) * P]
 
         def picked(window, lst, g):
             return window[:].indirect(entries(lst, g * PASS, PASS))
@@ -98,116 +101,134 @@ def tile_list_moment_centred_saved_placed_kernel(tc, xf, ra, gt, rb, sv, old, of
             nc.vector.tensor_reduce(total[:].rearrange("p b o -> p (b o)"),
                                     xg[:].rearrange("p (b m) -> p b m", m=GROUP), AXIS_X, ALU.add)
 
-        def centred_bank(xg, total, name):
-            minus_mean = held.tile([P, P], F32, name=name)
-            nc.vector.tensor_scalar(minus_mean[:].rearrange("p (b u) -> p b u", u=2),
-                                    total[:].to_broadcast([P, GROUPS, 2]), -1.0 / GROUP, None, ALU.mult)
+        def turned_features(xg):
             bank = turn.tile([P, PACK, P], F32, name="wide_bank")
             for t in range(PACK):
                 nc.tensor.matmul(bank[:, t, :], xg[:, t:PASS:PACK], ident[:], is_transpose=True,
                                  start=(t == 0), stop=False)
+            return bank
+
+        def centre(bank, total, minus_mean):
+            nc.vector.tensor_scalar(minus_mean[:].rearrange("p (b u) -> p b u", u=2),
+                                    total[:].to_broadcast([P, GROUPS, 2]), -1.0 / GROUP, None, ALU.mult)
             for t in range(PACK):
                 nc.tensor.matmul(bank[:, t, :], minus_mean[:], ident[:], is_transpose=True,
                                  start=False, stop=(t == PACK - 1))
-            return bank
 
         def weigh_features(g, bank, rounded):
             nc.vector.tensor_tensor(rounded[:].rearrange("p (c t) -> p c t", t=PACK), bank[:].rearrange("p t c -> p c t"),
                                     ra_slot[:, g:g + 1, :].to_broadcast([P, P, PACK]), ALU.mult)
 
-        def quantise(codes, scales, rounded):
+        def quantised(name, rounded, passes=1):
+            codes, scales = operand(name, passes)
             nc.vector.quantize_mx(out=codes[:].bitcast(E5M2X4), scales=scales[:], in_=rounded[:])
+            return codes, scales
 
-        def gated_bank(sg, weighted, gated):
+        def gate(sg, weighted, gated, halves):
             nc.vector.scalar_tensor_tensor(gated[:], sg[:], 0.0, weighted[:], ALU.max, ALU.mult)
             pairs = gated[:].bitcast(F32)
-            bank = turn.tile([P, 2, P], F32, name="pair_bank")
             for u in range(2):
-                nc.tensor.transpose(bank[:, u, :], pairs[:, u:PASS // 2:2], ident[:])
-            return bank
+                nc.tensor.transpose(halves[:, u, :], pairs[:, u:PASS // 2:2], ident[:])
 
-        def join_pairs(bank, name):
-            rounded = held.tile([P, PASS], BF16, name=name, align_bytes=64)
-            nc.scalar.copy(rounded[:].bitcast(F32).rearrange("p (c u) -> p c u", u=2), bank[:].rearrange("p u c -> p c u"))
-            return rounded
+        def join_pairs(bank, rounded):
+            nc.scalar.copy(rounded[:].bitcast(F32).rearrange("p (g c u) -> p g c u", c=P, u=2),
+                           bank[:].rearrange("p (g u) c -> p g c u", u=2))
 
-        def moment(i, n):
-            acc = sums_psum.tile([P, P], F32, name="acc%d%d" % (i, n))
-            for g in range(PASSES):
-                nc.tensor.matmul_mx(out=acc[:], lhsT=u_codes[i][g][:].bitcast(E5M2X4), lhsT_scale=u_scales[i][g][:],
-                                    rhs=g_codes[n][g][:].bitcast(E5M2X4), rhs_scale=g_scales[n][g][:],
-                                    start=(g == 0), stop=(g == PASSES - 1))
-            return acc
+        acc = [[sums_psum.tile([P, P], F32, name="acc%d%d" % (i, n)) for n in range(2)] for i in range(2)]
 
-        def place_on_scalar(i, n):
-            w = held.tile([P, P], F32, name="w%d%d" % (i, n))
-            nc.scalar.activation(w[:], moment(i, n)[:], COPY)
-            nc.scalar.activation(placed[i][:].indirect(entries(place_list, n * P, P)), w[:], COPY)
+        def moment_pass(i, n, g, features, gradients):
+            nc.tensor.matmul_mx(out=acc[i][n][:], lhsT=features[0].bitcast(E5M2X4), lhsT_scale=features[1],
+                                rhs=gradients[0].bitcast(E5M2X4), rhs_scale=gradients[1],
+                                start=(g == 0), stop=(g == PASSES - 1))
 
-        def place_on_vector(i, n):
-            w = held.tile([P, P], F32, name="w%d%d" % (i, n))
-            nc.vector.tensor_copy(w[:], moment(i, n)[:])
-            nc.vector.tensor_copy(placed[i][:].indirect(entries(place_list, n * P, P)), w[:])
+        def places(i, n):
+            return placed[i][:].indirect(entries(place_list, n * P, P))
 
+        mean0_at, rx0_at, mean1_at = spare + PIECE, spare + 2 * PIECE, spare + 4 * PIECE
         xg0 = [laid("xg00", [P, PASS], F32, spare), held.tile([P, PASS], F32, name="xg01")]
-        total0 = [laid("total00", [P, GROUPS, 1], F32, spare + PIECE), laid("total01", [P, GROUPS, 1], F32, x_at[0] + 3 * PIECE)]
+        total0 = [held.tile([P, GROUPS, 1], F32, name="total0%d" % g) for g in range(PASSES)]
+        minus_mean0 = [laid("minus_mean00", [P, P], F32, mean0_at), held.tile([P, P], F32, name="minus_mean01")]
+        rx0 = [laid("rx00", [P, PASS], BF16, rx0_at + PIECE // 2), laid("rx01", [P, PASS], BF16, rx0_at)]
+        gw0 = [laid("gw00", [P, PASS], F32, x_at[0] + 3 * PIECE), laid("gw01", [P, PASS], F32, g_at[0])]
+        gg0 = laid("gg0", [P, PASS], F32, x_at[0])
         nc.scalar.activation(xg0[0][:], picked(x_win[0], x_list, 0), COPY)
         nc.vector.tensor_copy(xg0[1][:], picked(x_win[0], x_list, 1))
+        x0 = {}
         for g in (1, 0):
             group_sums(xg0[g], total0[g])
-        x0 = {g: centred_bank(xg0[g], total0[g], "minus_mean0%d" % g) for g in (1, 0)}
-
-        gw0 = [laid("gw00", [P, PASS], F32, spare + PIECE), laid("gw01", [P, PASS], F32, g_at[0])]
-        gg0 = laid("gg0", [P, PASS], F32, x_at[0])
+            x0[g] = turned_features(xg0[g])
+        centre(x0[1], total0[1], minus_mean0[1])
         nc.vector.tensor_tensor(gw0[0][:], picked(g_win[0], g_list, 0), rb_row[0][:], ALU.mult)
         nc.scalar.activation(gg0[:], picked(g_win[0], g_list, 1), COPY)
-        rx0 = [held.tile([P, PASS], BF16, name="rx0%d" % g, align_bytes=64) for g in range(PASSES)]
-        for g in (1, 0):
-            weigh_features(g, x0[g], rx0[g])
-        for g in (1, 0):
-            quantise(u_codes[0][g], u_scales[0][g], rx0[g])
+        centre(x0[0], total0[0], minus_mean0[0])
+        weigh_features(1, x0[1], rx0[1])
         nc.vector.tensor_tensor(gw0[1][:], gg0[:], rb_row[1][:], ALU.mult)
+        weigh_features(0, x0[0], rx0[0])
 
         xg1 = [laid("xg1%d" % g, [P, PASS], F32, x_at[0] + (1 + g) * PIECE) for g in range(PASSES)]
-        total1 = [laid("total10", [P, GROUPS, 1], F32, g_at[0] + PIECE), held.tile([P, GROUPS, 1], F32, name="total11")]
-        x1 = []
+        total1 = [laid("total1%d" % g, [P, GROUPS, 1], F32, mean0_at + 4 * GROUPS * g) for g in range(PASSES)]
+        minus_mean1 = [held.tile([P, P], F32, name="minus_mean10"), laid("minus_mean11", [P, P], F32, mean1_at)]
         for g in range(PASSES):
             nc.scalar.activation(xg1[g][:], picked(x_win[1], x_list, g), COPY)
+        u0, x1 = {}, {}
         for g in range(PASSES):
+            u0[1 - g] = pass_of(quantised("u0%d" % (1 - g), rx0[1 - g]), 0)
             group_sums(xg1[g], total1[g])
-            x1.append(centred_bank(xg1[g], total1[g], "minus_mean1%d" % g))
+            x1[g] = turned_features(xg1[g])
+        centre(x1[0], total1[0], minus_mean1[0])
 
         sg0 = [laid("sg0%d" % g, [P, PASS], F32, x_at[1] + g * PIECE) for g in range(PASSES)]
         for g in range(PASSES):
             nc.scalar.activation(sg0[g][:], picked(s_win[0], g_list, g), COPY)
-        gated0 = [held.tile([P, PASS], BF16, name="gated00"), laid("gated01", [P, PASS], BF16, spare + 3 * PIECE - PIECE // 4)]
-        g0 = [gated_bank(sg0[0], gw0[0], gated0[0])]
-        gw1 = [laid("gw10", [P, PASS], F32, x_at[1]), held.tile([P, PASS], F32, name="gw11")]
+        gated0 = [laid("gated00", [P, PASS], BF16, rx0_at), laid("gated01", [P, PASS], BF16, x_at[1])]
+        gw1 = [laid("gw10", [P, PASS], F32, rx0_at + PIECE // 2), laid("gw11", [P, PASS], F32, x_at[0] + 3 * PIECE)]
+        gg1 = laid("gg1", [P, PASS], F32, x_at[1] + 3 * PIECE)
+        g0 = turn.tile([P, 2 * PASSES, P], F32, name="pair_bank")
+        gate(sg0[0], gw0[0], gated0[0], g0[:, 0:2, :])
+        centre(x1[1], total1[1], minus_mean1[1])
         nc.vector.tensor_tensor(gw1[0][:], picked(g_win[1], g_list, 0), rb_row[0][:], ALU.mult)
-        g0.append(gated_bank(sg0[1], gw0[1], gated0[1]))
-        gg1 = laid("gg1", [P, PASS], F32, x_at[1] + 2 * PIECE)
         nc.scalar.activation(gg1[:], picked(g_win[1], g_list, 1), COPY)
-        rg0 = [join_pairs(g0[g], "rg0%d" % g) for g in range(PASSES)]
-        rx10 = held.tile([P, PASS], BF16, name="rx10", align_bytes=64)
-        weigh_features(0, x1[0], rx10)
+        gate(sg0[1], gw0[1], gated0[1], g0[:, 2:4, :])
+        rx1 = [held.tile([P, PASS], BF16, name="rx1%d" % g, align_bytes=64) for g in range(PASSES)]
+        weigh_features(0, x1[0], rx1[0])
         nc.vector.tensor_tensor(gw1[1][:], gg1[:], rb_row[1][:], ALU.mult)
-        for g in range(PASSES):
-            quantise(g_codes[0][g], g_scales[0][g], rg0[g])
-        quantise(u_codes[1][0], u_scales[1][0], rx10)
+        u1 = [pass_of(quantised("u10", rx1[0]), 0)]
 
-        sg1 = [laid("sg1%d" % g, [P, PASS], F32, spare + (2 + g) * PIECE) for g in range(PASSES)]
+        sg1 = [laid("sg1%d" % g, [P, PASS], F32, s_at[0] + g * PIECE) for g in range(PASSES)]
         for g in range(PASSES):
             nc.scalar.activation(sg1[g][:], picked(s_win[1], g_list, g), COPY)
-        place_on_scalar(0, 0)
-        g1 = [gated_bank(sg1[g], gw1[g], held.tile([P, PASS], BF16, name="gated1%d" % g)) for g in range(PASSES)]
+        rg0 = laid("rg0", [P, J], BF16, s_at[1])
+        join_pairs(g0, rg0)
+        gated1 = [laid("gated10", [P, PASS], BF16, mean1_at), laid("gated11", [P, PASS], BF16, g_at[0] + 2 * PIECE)]
+        g1 = [turn.tile([P, 2, P], F32, name="pair_bank"), turn.tile([P, 2, P], F32, name="wide_bank")]
+        gate(sg1[0], gw1[0], gated1[0], g1[0][:])
+        weigh_features(1, x1[1], rx1[1])
+        gate(sg1[1], gw1[1], gated1[1], g1[1][:])
+        rg1 = [held.tile([P, PASS], BF16, name="rg10", align_bytes=64), laid("rg11", [P, PASS], BF16, g_at[0] + 3 * PIECE)]
         for g in range(PASSES):
-            quantise(g_codes[1][g], g_scales[1][g], join_pairs(g1[g], "rg1%d" % g))
-        rx11 = laid("rx11", [P, PASS], BF16, spare + 3 * PIECE)
-        weigh_features(1, x1[1], rx11)
-        quantise(u_codes[1][1], u_scales[1][1], rx11)
-        place_on_vector(0, 1)
-        place_on_scalar(1, 0)
-        place_on_scalar(1, 1)
+            join_pairs(g1[g], rg1[g])
+        u1.append(pass_of(quantised("u11", rx1[1]), 0))
+        u = [u0, u1]
+        v0 = quantised("v0", rg0, PASSES)
+        for i in range(2):
+            for g in range(PASSES):
+                moment_pass(i, 0, g, u[i][g], pass_of(v0, g))
+        v10 = pass_of(quantised("v10", rg1[0]), 0)
+        for i in range(2):
+            moment_pass(i, 1, 0, u[i][0], v10)
+        w = [[laid("w00", [P, P], F32, g_at[0] + 2 * PIECE), held.tile([P, P], F32, name="w01")],
+             [laid("w10", [P, P], F32, g_at[0] + 3 * PIECE), held.tile([P, P], F32, name="w11")]]
+        nc.vector.tensor_copy(w[0][0][:], acc[0][0][:])
+        nc.scalar.activation(places(0, 0), w[0][0][:], COPY)
+        v11 = pass_of(quantised("v11", rg1[1]), 0)
+        for i in range(2):
+            moment_pass(i, 1, 1, u[i][1], v11)
+        nc.vector.tensor_copy(w[1][0][:], acc[1][0][:])
+        nc.vector.tensor_copy(places(1, 0), w[1][0][:])
+        nc.scalar.activation(w[0][1][:], acc[0][1][:], COPY)
+        nc.scalar.activation(places(0, 1), w[0][1][:], COPY)
+        nc.vector.tensor_copy(w[1][1][:], acc[1][1][:])
+        nc.scalar.activation(places(1, 1), w[1][1][:], COPY)
 
         for i in range(2):
             for c in range(0, Q, HALF):

from contextlib import ExitStack

import concourse.mybir as mybir
from concourse.masks import make_identity

K, J, N, T, V, Q = 256, 1024, 256, 2048, 2048, 1024
FLOPS = 2 * K * J * N

F32 = mybir.dt.float32
BF16 = mybir.dt.bfloat16
U32 = mybir.dt.uint32
U16 = mybir.dt.uint16
U8 = mybir.dt.uint8
E5M2X4 = mybir.dt.float8_e5m2_x4
ALU = mybir.AluOpType
COPY = mybir.ActivationFunctionType.Copy
AXIS_X = mybir.AxisListType.X

P = 128
PACK = 4
PASS = P * PACK
PASSES = J // PASS
GROUP = 8
LANES = 16
STEP = 0.04
HALF = Q // 2
GROUPS = PASS // GROUP
WINDOW = 4 * T
PIECE = 4 * PASS


def tile_list_moment_centred_saved_placed_kernel(tc, xf, ra, gt, rb, sv, old, offs, offs2, offs3, out):
    nc = tc.nc
    with ExitStack() as ctx:
        held = ctx.enter_context(tc.tile_pool(name="held", bufs=1))
        reused = ctx.enter_context(tc.tile_pool(name="reused", bufs=1))
        turn = ctx.enter_context(tc.psum_pool(name="turn", bufs=2))
        sums_psum = ctx.enter_context(tc.psum_pool(name="sums_psum", bufs=1))

        def rows(i):
            return slice(i * P, (i + 1) * P)

        def entries(lst, start, count):
            return lst[:, start // LANES:(start + count) // LANES]

        def laid(name, shape, dtype, offset):
            return reused.tile(shape, dtype, name=name, offset=offset, align_bytes=64)

        x_list = held.tile([P, J // LANES], U16, name="x_list")
        g_list = held.tile([P, J // LANES], U16, name="g_list")
        place_list = held.tile([P, N // LANES], U16, name="place_list")
        x_at, g_at, s_at, spare = (0, 2 * WINDOW), (WINDOW, 4 * WINDOW), (3 * WINDOW, 5 * WINDOW), 6 * WINDOW
        x_win = [laid("x_win%d" % i, [P, T], F32, x_at[i]) for i in range(2)]
        g_win = [laid("g_win%d" % i, [P, V], F32, g_at[i]) for i in range(2)]
        s_win = [laid("s_win%d" % i, [P, V], F32, s_at[i]) for i in range(2)]
        store = [held.tile([P, Q], F32, name="store%d" % i) for i in range(2)]
        placed = [held.tile([P, Q], F32, name="placed%d" % i) for i in range(2)]
        ra_slot = held.tile([P, PASSES, PACK], F32, name="ra_slot")
        rb_slot = laid("rb_slot", [P, PASSES, PACK], F32, spare)
        ident = held.tile([P, P], F32, name="ident")

        nc.sync.dma_start(rb_slot[:], rb.rearrange("o (g p t) -> p (o g) t", g=PASSES, t=PACK))
        nc.sync.dma_start(x_list[:], offs)
        nc.sync.dma_start(x_win[0][:], xf[rows(0), :])
        nc.sync.dma_start(g_win[0][:], gt[rows(0), :])
        nc.sync.dma_start(g_list[:], offs2)
        nc.sync.dma_start(ra_slot[:], ra.rearrange("o (g p t) -> p (o g) t", g=PASSES, t=PACK))
        nc.sync.dma_start(x_win[1][:], xf[rows(1), :])
        nc.sync.dma_start(s_win[0][:], sv[rows(0), :])
        nc.sync.dma_start(g_win[1][:], gt[rows(1), :])
        nc.sync.dma_start(s_win[1][:], sv[rows(1), :])
        nc.sync.dma_start(place_list[:], offs3)
        for i in range(2):
            nc.sync.dma_start(store[i][:], old[rows(i), :])

        make_identity(nc, ident[:])
        for i in range(2):
            nc.vector.memset(placed[i][:], 0.0)

        def operand(name, passes):
            codes = held.tile([P, passes * P], U32, name=name + "_codes", align_bytes=64)
            scales = held.tile([P, passes * P], U8, name=name + "_scales", align_bytes=64)
            return codes, scales

        def pass_of(op, g):
            return op[0][:, g * P:(g + 1) * P], op[1][:, g * P:(g + 1) * P]

        def picked(window, lst, g):
            return window[:].indirect(entries(lst, g * PASS, PASS))

        rb_row = []
        for g in range(PASSES):
            bank = turn.tile([P, PACK, P], F32, name="wide_bank")
            for t in range(PACK):
                nc.tensor.transpose(bank[:, t, :], rb_slot[:, g, t:t + 1].to_broadcast([P, P]), ident[:])
            row = held.tile([P, PASS], F32, name="rb_row%d" % g)
            nc.scalar.activation(row[:].rearrange("p (c t) -> p c t", t=PACK), bank[:].rearrange("p t c -> p c t"), COPY)
            rb_row.append(row)

        def group_sums(xg, total):
            nc.vector.tensor_reduce(total[:].rearrange("p b o -> p (b o)"),
                                    xg[:].rearrange("p (b m) -> p b m", m=GROUP), AXIS_X, ALU.add)

        def turned_features(xg):
            bank = turn.tile([P, PACK, P], F32, name="wide_bank")
            for t in range(PACK):
                nc.tensor.matmul(bank[:, t, :], xg[:, t:PASS:PACK], ident[:], is_transpose=True,
                                 start=(t == 0), stop=False)
            return bank

        def centre(bank, total, minus_mean):
            nc.vector.tensor_scalar(minus_mean[:].rearrange("p (b u) -> p b u", u=2),
                                    total[:].to_broadcast([P, GROUPS, 2]), -1.0 / GROUP, None, ALU.mult)
            for t in range(PACK):
                nc.tensor.matmul(bank[:, t, :], minus_mean[:], ident[:], is_transpose=True,
                                 start=False, stop=(t == PACK - 1))

        def weigh_features(g, bank, rounded):
            nc.vector.tensor_tensor(rounded[:].rearrange("p (c t) -> p c t", t=PACK), bank[:].rearrange("p t c -> p c t"),
                                    ra_slot[:, g:g + 1, :].to_broadcast([P, P, PACK]), ALU.mult)

        def quantised(name, rounded, passes=1):
            codes, scales = operand(name, passes)
            nc.vector.quantize_mx(out=codes[:].bitcast(E5M2X4), scales=scales[:], in_=rounded[:])
            return codes, scales

        def gate(sg, weighted, gated, halves):
            nc.vector.scalar_tensor_tensor(gated[:], sg[:], 0.0, weighted[:], ALU.max, ALU.mult)
            pairs = gated[:].bitcast(F32)
            for u in range(2):
                nc.tensor.transpose(halves[:, u, :], pairs[:, u:PASS // 2:2], ident[:])

        def join_pairs(bank, rounded):
            nc.scalar.copy(rounded[:].bitcast(F32).rearrange("p (g c u) -> p g c u", c=P, u=2),
                           bank[:].rearrange("p (g u) c -> p g c u", u=2))

        acc = [[sums_psum.tile([P, P], F32, name="acc%d%d" % (i, n)) for n in range(2)] for i in range(2)]

        def moment_pass(i, n, g, features, gradients):
            nc.tensor.matmul_mx(out=acc[i][n][:], lhsT=features[0].bitcast(E5M2X4), lhsT_scale=features[1],
                                rhs=gradients[0].bitcast(E5M2X4), rhs_scale=gradients[1],
                                start=(g == 0), stop=(g == PASSES - 1))

        def places(i, n):
            return placed[i][:].indirect(entries(place_list, n * P, P))

        mean0_at, rx0_at, mean1_at = spare + PIECE, spare + 2 * PIECE, spare + 4 * PIECE
        xg0 = [laid("xg00", [P, PASS], F32, spare), held.tile([P, PASS], F32, name="xg01")]
        total0 = [held.tile([P, GROUPS, 1], F32, name="total0%d" % g) for g in range(PASSES)]
        minus_mean0 = [laid("minus_mean00", [P, P], F32, mean0_at), held.tile([P, P], F32, name="minus_mean01")]
        rx0 = [laid("rx00", [P, PASS], BF16, rx0_at + PIECE // 2), laid("rx01", [P, PASS], BF16, rx0_at)]
        gw0 = [laid("gw00", [P, PASS], F32, x_at[0] + 3 * PIECE), laid("gw01", [P, PASS], F32, g_at[0])]
        gg0 = laid("gg0", [P, PASS], F32, x_at[0])
        nc.scalar.activation(xg0[0][:], picked(x_win[0], x_list, 0), COPY)
        nc.vector.tensor_copy(xg0[1][:], picked(x_win[0], x_list, 1))
        x0 = {}
        for g in (1, 0):
            group_sums(xg0[g], total0[g])
            x0[g] = turned_features(xg0[g])
        centre(x0[1], total0[1], minus_mean0[1])
        nc.vector.tensor_tensor(gw0[0][:], picked(g_win[0], g_list, 0), rb_row[0][:], ALU.mult)
        nc.scalar.activation(gg0[:], picked(g_win[0], g_list, 1), COPY)
        centre(x0[0], total0[0], minus_mean0[0])
        weigh_features(1, x0[1], rx0[1])
        nc.vector.tensor_tensor(gw0[1][:], gg0[:], rb_row[1][:], ALU.mult)
        weigh_features(0, x0[0], rx0[0])

        xg1 = [laid("xg1%d" % g, [P, PASS], F32, x_at[0] + (1 + g) * PIECE) for g in range(PASSES)]
        total1 = [laid("total1%d" % g, [P, GROUPS, 1], F32, mean0_at + 4 * GROUPS * g) for g in range(PASSES)]
        minus_mean1 = [held.tile([P, P], F32, name="minus_mean10"), laid("minus_mean11", [P, P], F32, mean1_at)]
        for g in range(PASSES):
            nc.scalar.activation(xg1[g][:], picked(x_win[1], x_list, g), COPY)
        u0, x1 = {}, {}
        for g in range(PASSES):
            u0[1 - g] = pass_of(quantised("u0%d" % (1 - g), rx0[1 - g]), 0)
            group_sums(xg1[g], total1[g])
            x1[g] = turned_features(xg1[g])
        centre(x1[0], total1[0], minus_mean1[0])

        sg0 = [laid("sg0%d" % g, [P, PASS], F32, x_at[1] + g * PIECE) for g in range(PASSES)]
        for g in range(PASSES):
            nc.scalar.activation(sg0[g][:], picked(s_win[0], g_list, g), COPY)
        gated0 = [laid("gated00", [P, PASS], BF16, rx0_at), laid("gated01", [P, PASS], BF16, x_at[1])]
        gw1 = [laid("gw10", [P, PASS], F32, rx0_at + PIECE // 2), laid("gw11", [P, PASS], F32, x_at[0] + 3 * PIECE)]
        gg1 = laid("gg1", [P, PASS], F32, x_at[1] + 3 * PIECE)
        g0 = turn.tile([P, 2 * PASSES, P], F32, name="pair_bank")
        gate(sg0[0], gw0[0], gated0[0], g0[:, 0:2, :])
        centre(x1[1], total1[1], minus_mean1[1])
        nc.vector.tensor_tensor(gw1[0][:], picked(g_win[1], g_list, 0), rb_row[0][:], ALU.mult)
        nc.scalar.activation(gg1[:], picked(g_win[1], g_list, 1), COPY)
        gate(sg0[1], gw0[1], gated0[1], g0[:, 2:4, :])
        rx1 = [held.tile([P, PASS], BF16, name="rx1%d" % g, align_bytes=64) for g in range(PASSES)]
        weigh_features(0, x1[0], rx1[0])
        nc.vector.tensor_tensor(gw1[1][:], gg1[:], rb_row[1][:], ALU.mult)
        u1 = [pass_of(quantised("u10", rx1[0]), 0)]

        sg1 = [laid("sg1%d" % g, [P, PASS], F32, s_at[0] + g * PIECE) for g in range(PASSES)]
        for g in range(PASSES):
            nc.scalar.activation(sg1[g][:], picked(s_win[1], g_list, g), COPY)
        rg0 = laid("rg0", [P, J], BF16, s_at[1])
        join_pairs(g0, rg0)
        gated1 = [laid("gated10", [P, PASS], BF16, mean1_at), laid("gated11", [P, PASS], BF16, g_at[0] + 2 * PIECE)]
        g1 = [turn.tile([P, 2, P], F32, name="pair_bank"), turn.tile([P, 2, P], F32, name="wide_bank")]
        gate(sg1[0], gw1[0], gated1[0], g1[0][:])
        weigh_features(1, x1[1], rx1[1])
        gate(sg1[1], gw1[1], gated1[1], g1[1][:])
        rg1 = [held.tile([P, PASS], BF16, name="rg10", align_bytes=64), laid("rg11", [P, PASS], BF16, g_at[0] + 3 * PIECE)]
        for g in range(PASSES):
            join_pairs(g1[g], rg1[g])
        u1.append(pass_of(quantised("u11", rx1[1]), 0))
        u = [u0, u1]
        v0 = quantised("v0", rg0, PASSES)
        for i in range(2):
            for g in range(PASSES):
                moment_pass(i, 0, g, u[i][g], pass_of(v0, g))
        v10 = pass_of(quantised("v10", rg1[0]), 0)
        for i in range(2):
            moment_pass(i, 1, 0, u[i][0], v10)
        w = [[laid("w00", [P, P], F32, g_at[0] + 2 * PIECE), held.tile([P, P], F32, name="w01")],
             [laid("w10", [P, P], F32, g_at[0] + 3 * PIECE), held.tile([P, P], F32, name="w11")]]
        nc.vector.tensor_copy(w[0][0][:], acc[0][0][:])
        nc.scalar.activation(places(0, 0), w[0][0][:], COPY)
        v11 = pass_of(quantised("v11", rg1[1]), 0)
        for i in range(2):
            moment_pass(i, 1, 1, u[i][1], v11)
        nc.vector.tensor_copy(w[1][0][:], acc[1][0][:])
        nc.vector.tensor_copy(places(1, 0), w[1][0][:])
        nc.scalar.activation(w[0][1][:], acc[0][1][:], COPY)
        nc.scalar.activation(places(0, 1), w[0][1][:], COPY)
        nc.vector.tensor_copy(w[1][1][:], acc[1][1][:])
        nc.scalar.activation(places(1, 1), w[1][1][:], COPY)

        for i in range(2):
            for c in range(0, Q, HALF):
                cols = slice(c, c + HALF)
                nc.vector.scalar_tensor_tensor(store[i][:, cols], placed[i][:, cols], STEP, store[i][:, cols],
                                               ALU.mult, ALU.add)
                nc.sync.dma_start(out[rows(i), cols], store[i][:, cols])
